import numpy as np
import ml_dtypes


def mxq(x, axis, fmt="e4m3"):
    dtype, down = {"e4m3": (ml_dtypes.float8_e4m3fn, 7), "e5m2": (ml_dtypes.float8_e5m2, 14)}[fmt]
    v = np.moveaxis(np.asarray(x, np.float32).astype(ml_dtypes.bfloat16).astype(np.float64), axis, -1)
    blocks = v.reshape(v.shape[:-1] + (-1, 32))
    amax = np.abs(blocks).max(-1, keepdims=True)
    byte = np.maximum(np.where(amax > 0, np.frexp(amax)[1] - 1 + 127, 0) - down, 1)
    scale = np.exp2(byte - 127.0)
    codes = (blocks / scale).astype(np.float32).astype(dtype).astype(np.float64)
    return np.moveaxis((codes * scale).reshape(v.shape), -1, axis)


WIDE = False


def mx_kscale(k):
    if not WIDE:
        return np.ones(k)
    levels = np.array([18, -18])
    if k % 512:
        return np.exp2(np.random.permutation(np.resize(levels, k // 32))).repeat(32)
    a = np.empty((k // 512, 16))
    for p in range(k // 512):
        a[p, :8] = np.random.permutation(np.resize(levels, 8))
        for g in range(8):
            far = levels[np.abs(levels - a[p, g]) >= 10]
            a[p, g + 8] = far[np.random.randint(len(far))]
    return np.exp2(a.ravel()).repeat(32)


def f64(x):
    return np.asarray(x).astype(np.float64)


def striped(idx):
    return np.tile(np.asarray(idx).reshape(-1, 16).T, (8, 1)).astype(np.uint16)


def unstriped(offs):
    return offs[:16].T.reshape(-1).astype(np.int64)


E2M1 = np.array([0.0, 0.5, 1.0, 1.5, 2.0, 3.0, 4.0, 6.0, -0.0, -0.5, -1.0, -1.5, -2.0, -3.0, -4.0, -6.0])


def pack_weight(w, fmt):
    k, n = w.shape
    w = f64(np.asarray(w, np.float32).astype(ml_dtypes.bfloat16)).reshape(k // 32, 32, n)
    amax = np.abs(w).max(1)
    if fmt == "e4m3":
        byte = np.frexp(amax)[1] - 1 + 127 - 7
    else:
        mant, ex = np.frexp(amax / 6.0)
        byte = np.where(mant > 0.5, ex, ex - 1) + 127
    byte = np.clip(np.where(amax > 0, byte, 1), 1, 254)
    scaled = (w * np.exp2(127.0 - byte)[:, None, :]).reshape(k, n).astype(np.float32)
    by_word = np.ascontiguousarray(scaled.reshape(k // 512, 128, 4, n).transpose(0, 1, 3, 2))
    if fmt == "e4m3":
        words = by_word.astype(ml_dtypes.float8_e4m3fn).view(np.uint8)
    else:
        c = by_word.astype(ml_dtypes.float4_e2m1fn).view(np.uint8) & 0xF
        words = (c[..., 0::2] | (c[..., 1::2] << 4)).reshape(k // 512, 128, 2 * n)
    return np.ascontiguousarray(words), np.ascontiguousarray(byte.astype(np.uint8).reshape(k // 512, 16, n))


def unpack_weight(words, scales, fmt):
    g, _, n = scales.shape
    words = np.ascontiguousarray(words).reshape(g, 128, n, -1)
    if fmt == "e4m3":
        vals = words.view(ml_dtypes.float8_e4m3fn).astype(np.float64)
    else:
        nib = np.empty((g, 128, n, 4), np.uint8)
        nib[..., 0::2] = words & 0xF
        nib[..., 1::2] = words >> 4
        vals = E2M1[nib]
    vals = vals * np.repeat(np.exp2(scales.astype(np.float64) - 127.0), 8, axis=1)[..., None]
    return vals.transpose(0, 1, 3, 2).reshape(g * 512, n)


def planes(y):
    n, m = y.shape
    v = y.astype(np.float32).astype(ml_dtypes.bfloat16).astype(np.float64).reshape(n // 32, 32, m)
    top = np.abs(v).max(1)
    byte = np.clip(np.where(top > 0, np.frexp(top)[1] - 1 + 127 - 7, 1), 1, 254)
    codes = (v * np.exp2(127.0 - byte)[:, None, :]).reshape(n, m).astype(np.float32).astype(ml_dtypes.float8_e4m3fn).view(np.uint8)
    words = codes.reshape(n // 512, 128, 4, m).transpose(0, 1, 3, 2)
    return np.ascontiguousarray(words), np.ascontiguousarray(byte.astype(np.uint8).reshape(n // 512, 16, m))


def setup_inputs():
    n = np.random.standard_normal
    uni = np.random.uniform
    idx = np.random.permutation(1024)[:512]
    f_h = mx_kscale(512)
    f_m = mx_kscale(512)
    U_ = pack_weight(n((512, 512)) / np.sqrt(512) / f_h[:, None], "e4m3")
    return {
        "dy": (n((512, 512)) * f_m[:, None]).astype(np.float32),
        "wo": (n((512, 512)) / np.sqrt(512) / f_m[:, None] * f_h[None, :]).astype(np.float32),
        "dn": (n((512, 1024)) * f_h[:, None]).astype(np.float32),
        "hT": (np.tanh(1.5 * n((512, 1024)))).astype(np.float32),
        "U_words": U_[0],
        "U_scales": U_[1],
        "offs": striped(idx),
    }


def reference(dy, wo, dn, hT, U_words, U_scales, offs):
    idx = unstriped(offs)
    dn_ = f64(dn)[:, idx]
    h_ = f64(hT)[:, idx]
    U = unpack_weight(U_words, U_scales, "e4m3")
    a = mxq(f64(wo), 0, "e4m3").T @ mxq(f64(dy), 0, "e5m2")
    z = (a + dn_) * (1.0 - np.square(h_))
    dh = U.T @ mxq(z, 0, "e5m2")
    out_0 = np.zeros((512, 1024))
    out_0[:, idx] = dh
    return (out_0,) + planes(out_0)

@@ -1,0 +1,218 @@
+from contextlib import ExitStack
+
+import concourse.mybir as mybir
+
+F32 = mybir.dt.float32
+BF16 = mybir.dt.bfloat16
+I32 = mybir.dt.int32
+U16 = mybir.dt.uint16
+U8 = mybir.dt.uint8
+E4M3 = mybir.dt.float8_e4m3fn_x4
+E5M2 = mybir.dt.float8_e5m2_x4
+ALU = mybir.AluOpType
+ACT = mybir.ActivationFunctionType
+
+P = 128
+LANES = 4
+D = 512
+SLOTS = 512
+SESSIONS = 1024
+FLOPS = 2 * 2 * D * D * SLOTS
+
+WO_VECTOR = 88
+DY_VECTOR = 352
+TAIL_VECTOR = 512
+CHUNK = 256
+
+
+def tile_attend_grnn_pl_kernel(tc, dy, wo, dn, hT, U_words, U_scales, offs, out_0, out_1, out_2):
+    nc = tc.nc
+    with ExitStack() as ctx:
+        sb = ctx.enter_context(tc.tile_pool(name="sb", bufs=1))
+        ps = ctx.enter_context(tc.psum_pool(name="ps", bufs=1))
+
+        def tile(name, shape, dtype, tag=None):
+            return sb.tile(shape, dtype, name=name, tag=tag or name, align_bytes=64)
+
+        offsets = sb.tile([P, SLOTS // 16], U16, name="offsets")
+        nc.sync.dma_start(offsets[:], offs)
+
+        wo_raw = tile("wo_raw", [P, LANES, D], F32)
+        nc.sync.dma_start(wo_raw[:], wo.rearrange("(p j) h -> p j h", j=LANES))
+        us_raw = tile("us_raw", [P, D], U8)
+        nc.vector.memset(us_raw[:].bitcast(I32), 0)
+        for q in range(4):
+            nc.scalar.dma_start(us_raw[32 * q : 32 * q + 4, :].bitcast(I32), U_scales[0, 4 * q : 4 * q + 4, :].bitcast(I32))
+        dy_raw = tile("dy_raw", [P, LANES, SLOTS], F32)
+        nc.sync.dma_start(dy_raw[:], dy.rearrange("(p j) i -> p j i", j=LANES))
+
+        h_rows = hT.rearrange("(p t) c -> p t c", t=LANES)
+        dn_rows = dn.rearrange("(p t) c -> p t c", t=LANES)
+        h_tab = [tile("h_tab%d" % t, [P, SESSIONS], F32) for t in range(LANES)]
+        dn_tab = [tile("dn_tab%d" % t, [P, SESSIONS], F32) for t in range(LANES)]
+        u_raw = tile("u_raw", [P, D], I32)
+        for t in range(LANES):
+            nc.sync.dma_start(h_tab[t][:], h_rows[:, t, :])
+            if t == 0:
+                nc.sync.dma_start(u_raw[:], U_words[0].rearrange("p k l -> p (k l)").bitcast(I32))
+            nc.sync.dma_start(dn_tab[t][:], dn_rows[:, t, :])
+
+        window = [tile("window%d" % t, [P, SESSIONS], F32) for t in range(LANES)]
+        for t in range(LANES):
+            nc.vector.memset(window[t][:], 0.0)
+
+        u_scale = tile("u_scale", [P, LANES, P], U8)
+        nc.vector.tensor_copy(u_scale[:].rearrange("p t m -> p m t"), us_raw[:].rearrange("p (m t) -> p m t", t=LANES))
+
+        wo_bf = tile("wo_bf", [P, LANES, P, LANES], BF16)
+        wo_dst = wo_bf[:].rearrange("p t m j -> p m t j")
+        wo_src = wo_raw[:].rearrange("p j (m t) -> p m t j", t=LANES)
+        nc.vector.tensor_copy(wo_dst[:, :WO_VECTOR], wo_src[:, :WO_VECTOR])
+        nc.scalar.copy(wo_dst[:, WO_VECTOR:], wo_src[:, WO_VECTOR:])
+        wo_code = tile("wo_code", [P, D], I32)
+        wo_scale = tile("wo_scale", [P, D], U8)
+        nc.vector.quantize_mx(wo_code[:].bitcast(E4M3), wo_scale[:], wo_bf[:].rearrange("p t m j -> p (t m j)"))
+
+        dy_bf = tile("dy_bf", [P, SLOTS, LANES], BF16)
+        dy_src = dy_raw[:].rearrange("p j i -> p i j")
+        half = SLOTS // 2
+        nc.scalar.copy(dy_bf[:, DY_VECTOR:], dy_src[:, DY_VECTOR:])
+        nc.vector.tensor_copy(dy_bf[:, :half], dy_src[:, :half])
+        nc.vector.tensor_copy(dy_bf[:, half:DY_VECTOR], dy_src[:, half:DY_VECTOR])
+        grad_code = tile("grad_code", [P, 2 * SLOTS], I32)
+        grad_scale = tile("grad_scale", [P, 2 * SLOTS], U8)
+        for c in (0, half):
+            cols = slice(c, c + half)
+            nc.vector.quantize_mx(grad_code[:, cols].bitcast(E5M2), grad_scale[:, cols], dy_bf[:, cols, :].rearrange("p i j -> p (i j)"))
+
+        first, second, whole = slice(0, half), slice(half, SLOTS), slice(0, SLOTS)
+
+        def listed(table, part):
+            return table[:].indirect(offsets[:, part.start // 16 : part.stop // 16])
+
+        def label(name, t, part):
+            return "%s%d_%d_%d" % (name, t, part.start, part.stop)
+
+        def product_mx(name, code, scale, start):
+            acc = ps.tile([P, SLOTS], F32, name=name, tag="bank", bufs=8)
+            cols = slice(start, start + SLOTS)
+            nc.tensor.matmul_mx(acc[:], lhsT=code.bitcast(E4M3), lhsT_scale=scale,
+                                rhs=grad_code[:, cols].bitcast(E5M2), rhs_scale=grad_scale[:, cols], start=True, stop=True)
+            return acc
+
+        parts = [[whole], [whole], [first, second], [first, second]]
+        a_sb = {}
+        for t in range(LANES):
+            cols = slice(P * t, P * (t + 1))
+            acc = product_mx("a_ps%d" % t, wo_code[:, cols], wo_scale[:, cols], 0)
+            for part in parts[t]:
+                a_t = tile(label("a", t, part), [P, part.stop - part.start], F32)
+                nc.scalar.copy(a_t[:], acc[:, part])
+                a_sb[t, part.start] = a_t
+
+        u_code = tile("u_code", [P, LANES, P], I32)
+        z_plane = [tile("z_plane%d" % c, [P, LANES, half], BF16) for c in range(2)]
+        h_sq = {}
+        total = {}
+
+        def gather_h(t, part, tag=None):
+            width = part.stop - part.start
+            h_t = tile(label("h", t, part), [P, width], F32, tag)
+            nc.vector.tensor_copy(h_t[:], listed(h_tab[t], part))
+            sq = tile(label("h_sq", t, part), [P, width], F32)
+            nc.scalar.activation(sq[:], h_t[:], ACT.Square)
+            for c in range(part.start, part.stop, half):
+                h_sq[t, c] = sq[:, c - part.start : c - part.start + half]
+
+        def gather_dn(t, part, tag=None):
+            s = tile(label("total", t, part), [P, part.stop - part.start], F32, tag)
+            nc.vector.tensor_tensor(s[:], listed(dn_tab[t], part), a_sb[t, part.start][:], ALU.add)
+            for c in range(part.start, part.stop, half):
+                total[t, c] = s[:, c - part.start : c - part.start + half]
+
+        def product(t, c):
+            nc.vector.scalar_tensor_tensor(z_plane[c // half][:, t, :], h_sq[t, c], 1.0, total[t, c], ALU.subtract, ALU.mult)
+
+        def weave_z(c):
+            z_bf = tile("z_bf%d" % c, [P, half, LANES], BF16)
+            nc.scalar.copy(z_bf[:], z_plane[c // half][:].rearrange("p t i -> p i t"))
+            return z_bf
+
+        def quantise_z(c, z_bf):
+            cols = slice(SLOTS + c, SLOTS + c + half)
+            nc.vector.quantize_mx(grad_code[:, cols].bitcast(E5M2), grad_scale[:, cols], z_bf[:].rearrange("p i t -> p (i t)"))
+
+        gather_h(0, whole, "dy_bf")
+        nc.vector.tensor_copy(u_code[:].rearrange("p t m -> p m t"), u_raw[:].rearrange("p (m t) -> p m t", t=LANES))
+        for t in range(2):
+            gather_dn(t, whole)
+            gather_h(t + 1, whole)
+            product(t, 0)
+            product(t, half)
+        gather_dn(2, first)
+        gather_h(3, first)
+        product(2, 0)
+        gather_dn(3, first)
+        product(3, 0)
+        z_first = weave_z(0)
+        gather_h(3, second, label("a", 3, first))
+        gather_dn(2, second, label("total", 3, first))
+        product(2, half)
+        quantise_z(0, z_first)
+        gather_dn(3, second, "z_bf0")
+        product(3, half)
+
+        minus_one = tile("minus_one", [P, 1], F32)
+        nc.vector.memset(minus_one[:], -1.0)
+
+        def negated(t, part, acc, cols, tag=None):
+            dh_t = tile(label("dh", t, part), [P, part.stop - part.start], F32, tag)
+            nc.scalar.activation(dh_t[:], acc[:, cols], ACT.Copy, scale=minus_one[:])
+            return dh_t
+
+        def scatter(t, part, dh_t):
+            nc.vector.tensor_copy(listed(window[t], part), dh_t[:])
+
+        early = [product_mx("early%d" % t, u_code[:, t, :], u_scale[:, t, :], half) for t in range(2)]
+        dh_0 = negated(0, first, early[0], second)
+        z_second = weave_z(half)
+        dh_1 = negated(1, first, early[1], second, "z_plane1")
+        scatter(0, first, dh_0)
+        quantise_z(half, z_second)
+        scatter(1, first, dh_1)
+
+        rest = [second, second, whole, whole]
+        dh = []
+        for t in range(LANES):
+            acc = product_mx("dh_ps%d" % t, u_code[:, t, :], u_scale[:, t, :], SLOTS)
+            dh.append(negated(t, rest[t], acc, rest[t]))
+
+        out_rows = out_0.rearrange("(p t) c -> p t c", t=LANES)
+        y_bf = tile("y_bf", [P, SESSIONS, LANES], BF16, "minus_one")
+        y_pair = tile("y_pair", [P, 2, TAIL_VECTOR], BF16)
+        for t in range(LANES):
+            scatter(t, rest[t], dh[t])
+            nc.sync.dma_start(out_rows[:, t, :], window[t][:])
+            if t < 2:
+                nc.scalar.copy(y_bf[:, :, t], window[t][:])
+            if t == 2:
+                nc.scalar.copy(y_pair[:, 0, :], window[t][:, :TAIL_VECTOR])
+                nc.scalar.copy(y_bf[:, TAIL_VECTOR:, t], window[t][:, TAIL_VECTOR:])
+
+        last = window[LANES - 1]
+        nc.vector.tensor_copy(y_pair[:, 1, :], last[:, :TAIL_VECTOR])
+        for c in range(TAIL_VECTOR, SESSIONS, CHUNK):
+            nc.scalar.copy(y_bf[:, c : c + CHUNK, LANES - 1], last[:, c : c + CHUNK])
+        for c in range(0, TAIL_VECTOR, CHUNK):
+            nc.vector.tensor_copy(y_bf[:, c : c + CHUNK, 2:4], y_pair[:, :, c : c + CHUNK].rearrange("p t c -> p c t"))
+
+        y_code = tile("y_code", [P, SESSIONS], I32)
+        y_scale = tile("y_scale", [P, SESSIONS], U8)
+        word_rows = out_1[0].rearrange("p c l -> p (c l)").bitcast(I32)
+        for c in (2 * CHUNK, 0, CHUNK, 3 * CHUNK):
+            cols = slice(c, c + CHUNK)
+            nc.vector.quantize_mx(y_code[:, cols].bitcast(E4M3), y_scale[:, cols], y_bf[:, cols, :].rearrange("p c t -> p (c t)"))
+            nc.sync.dma_start(word_rows[:, cols], y_code[:, cols])
+        for q in range(4):
+            queue = nc.scalar if q % 2 else nc.sync
+            queue.dma_start(out_2[0, 4 * q : 4 * q + 4, :].bitcast(I32), y_scale[32 * q : 32 * q + 4, :].bitcast(I32))

@@ -40,7 +40,7 @@ def tile_attend_grnn_pl_kernel(tc, dy, wo, dn, hT, U_words, U_scales, offs, out_
         wo_raw = tile("wo_raw", [P, LANES, D], F32)
         nc.sync.dma_start(wo_raw[:], wo.rearrange("(p j) h -> p j h", j=LANES))
         us_raw = tile("us_raw", [P, D], U8)
-        nc.vector.memset(us_raw[:].bitcast(I32), 0)
+        nc.gpsimd.memset(us_raw[:].bitcast(I32), 0)
         for q in range(4):
             nc.scalar.dma_start(us_raw[32 * q : 32 * q + 4, :].bitcast(I32), U_scales[0, 4 * q : 4 * q + 4, :].bitcast(I32))
         dy_raw = tile("dy_raw", [P, LANES, SLOTS], F32)
@@ -61,9 +61,6 @@ def tile_attend_grnn_pl_kernel(tc, dy, wo, dn, hT, U_words, U_scales, offs, out_
         for t in range(LANES):
             nc.vector.memset(window[t][:], 0.0)
 
-        u_scale = tile("u_scale", [P, LANES, P], U8)
-        nc.vector.tensor_copy(u_scale[:].rearrange("p t m -> p m t"), us_raw[:].rearrange("p (m t) -> p m t", t=LANES))
-
         wo_bf = tile("wo_bf", [P, LANES, P, LANES], BF16)
         wo_dst = wo_bf[:].rearrange("p t m j -> p m t j")
         wo_src = wo_raw[:].rearrange("p j (m t) -> p m t j", t=LANES)
@@ -72,6 +69,9 @@ def tile_attend_grnn_pl_kernel(tc, dy, wo, dn, hT, U_words, U_scales, offs, out_
         wo_code = tile("wo_code", [P, D], I32)
         wo_scale = tile("wo_scale", [P, D], U8)
         nc.vector.quantize_mx(wo_code[:].bitcast(E4M3), wo_scale[:], wo_bf[:].rearrange("p t m j -> p (t m j)"))
+
+        u_scale = tile("u_scale", [P, LANES, P], U8, "wo_bf")
+        nc.vector.tensor_copy(u_scale[:].rearrange("p t m -> p m t"), us_raw[:].rearrange("p (m t) -> p m t", t=LANES))
 
         dy_bf = tile("dy_bf", [P, SLOTS, LANES], BF16)
         dy_src = dy_raw[:].rearrange("p j i -> p i j")
@@ -162,12 +162,9 @@ def tile_attend_grnn_pl_kernel(tc, dy, wo, dn, hT, U_words, U_scales, offs, out_
         gather_dn(3, second, "z_bf0")
         product(3, half)
 
-        minus_one = tile("minus_one", [P, 1], F32)
-        nc.vector.memset(minus_one[:], -1.0)
-
         def negated(t, part, acc, cols, tag=None):
             dh_t = tile(label("dh", t, part), [P, part.stop - part.start], F32, tag)
-            nc.scalar.activation(dh_t[:], acc[:, cols], ACT.Copy, scale=minus_one[:])
+            nc.scalar.activation(dh_t[:], acc[:, cols], ACT.Copy, scale=-1.0)
             return dh_t
 
         def scatter(t, part, dh_t):
@@ -188,13 +185,20 @@ def tile_attend_grnn_pl_kernel(tc, dy, wo, dn, hT, U_words, U_scales, offs, out_
             dh.append(negated(t, rest[t], acc, rest[t]))
 
         out_rows = out_0.rearrange("(p t) c -> p t c", t=LANES)
-        y_bf = tile("y_bf", [P, SESSIONS, LANES], BF16, "minus_one")
-        y_pair = tile("y_pair", [P, 2, TAIL_VECTOR], BF16)
+        y_bf = tile("y_bf", [P, SESSIONS, LANES], BF16, "wo_bf")
+        y_low = tile("y_low", [P, 2, SESSIONS], BF16, "u_code")
+        y_pair = tile("y_pair", [P, 2, TAIL_VECTOR], BF16, "grad_scale")
         for t in range(LANES):
             scatter(t, rest[t], dh[t])
             nc.sync.dma_start(out_rows[:, t, :], window[t][:])
-            if t < 2:
-                nc.scalar.copy(y_bf[:, :, t], window[t][:])
+            if t == 0:
+                nc.scalar.copy(y_low[:, t, :], window[t][:])
+            if t == 1:
+                sides = (slice(0, SESSIONS // 2), slice(SESSIONS // 2, SESSIONS))
+                for cols in sides:
+                    nc.scalar.copy(y_low[:, t, cols], window[t][:, cols])
+                for cols in sides:
+                    nc.scalar.copy(y_bf[:, cols, 0:2], y_low[:, :, cols].rearrange("p t c -> p c t"))
             if t == 2:
                 nc.scalar.copy(y_pair[:, 0, :], window[t][:, :TAIL_VECTOR])
                 nc.scalar.copy(y_bf[:, TAIL_VECTOR:, t], window[t][:, TAIL_VECTOR:])

@@ -21,7 +21,7 @@ FLOPS = 2 * 2 * D * D * SLOTS
 
 WO_VECTOR = 88
 DY_VECTOR = 352
-TAIL_VECTOR = 512
+TAIL_VECTOR = 448
 CHUNK = 256
 
 
@@ -43,18 +43,19 @@ def tile_attend_grnn_pl_kernel(tc, dy, wo, dn, hT, U_words, U_scales, offs, out_
         nc.gpsimd.memset(us_raw[:].bitcast(I32), 0)
         for q in range(4):
             nc.scalar.dma_start(us_raw[32 * q : 32 * q + 4, :].bitcast(I32), U_scales[0, 4 * q : 4 * q + 4, :].bitcast(I32))
-        dy_raw = tile("dy_raw", [P, LANES, SLOTS], F32)
-        nc.sync.dma_start(dy_raw[:], dy.rearrange("(p j) i -> p j i", j=LANES))
+        dy_rows = dy.rearrange("(p j) i -> p j i", j=LANES)
+        dy_raw = [tile("dy_raw%d" % u, [P, 2, SLOTS], F32) for u in range(2)]
+        for u in range(2):
+            nc.sync.dma_start(dy_raw[u][:], dy_rows[:, 2 * u : 2 * u + 2, :])
 
         h_rows = hT.rearrange("(p t) c -> p t c", t=LANES)
         dn_rows = dn.rearrange("(p t) c -> p t c", t=LANES)
         h_tab = [tile("h_tab%d" % t, [P, SESSIONS], F32) for t in range(LANES)]
         dn_tab = [tile("dn_tab%d" % t, [P, SESSIONS], F32) for t in range(LANES)]
         u_raw = tile("u_raw", [P, D], I32)
+        nc.sync.dma_start(u_raw[:], U_words[0].rearrange("p k l -> p (k l)").bitcast(I32))
         for t in range(LANES):
             nc.sync.dma_start(h_tab[t][:], h_rows[:, t, :])
-            if t == 0:
-                nc.sync.dma_start(u_raw[:], U_words[0].rearrange("p k l -> p (k l)").bitcast(I32))
             nc.sync.dma_start(dn_tab[t][:], dn_rows[:, t, :])
 
         window = [tile("window%d" % t, [P, SESSIONS], F32) for t in range(LANES)]
@@ -74,11 +75,13 @@ def tile_attend_grnn_pl_kernel(tc, dy, wo, dn, hT, U_words, U_scales, offs, out_
         nc.vector.tensor_copy(u_scale[:].rearrange("p t m -> p m t"), us_raw[:].rearrange("p (m t) -> p m t", t=LANES))
 
         dy_bf = tile("dy_bf", [P, SLOTS, LANES], BF16)
-        dy_src = dy_raw[:].rearrange("p j i -> p i j")
         half = SLOTS // 2
-        nc.scalar.copy(dy_bf[:, DY_VECTOR:], dy_src[:, DY_VECTOR:])
-        nc.vector.tensor_copy(dy_bf[:, :half], dy_src[:, :half])
-        nc.vector.tensor_copy(dy_bf[:, half:DY_VECTOR], dy_src[:, half:DY_VECTOR])
+        for u in range(2):
+            dy_src = dy_raw[u][:].rearrange("p j i -> p i j")
+            lanes = slice(2 * u, 2 * u + 2)
+            nc.scalar.copy(dy_bf[:, DY_VECTOR:, lanes], dy_src[:, DY_VECTOR:])
+            nc.vector.tensor_copy(dy_bf[:, :half, lanes], dy_src[:, :half])
+            nc.vector.tensor_copy(dy_bf[:, half:DY_VECTOR, lanes], dy_src[:, half:DY_VECTOR])
         grad_code = tile("grad_code", [P, 2 * SLOTS], I32)
         grad_scale = tile("grad_scale", [P, 2 * SLOTS], U8)
         for c in (0, half):
@@ -100,33 +103,34 @@ def tile_attend_grnn_pl_kernel(tc, dy, wo, dn, hT, U_words, U_scales, offs, out_
                                 rhs=grad_code[:, cols].bitcast(E5M2), rhs_scale=grad_scale[:, cols], start=True, stop=True)
             return acc
 
-        parts = [[whole], [whole], [first, second], [first, second]]
         a_sb = {}
         for t in range(LANES):
             cols = slice(P * t, P * (t + 1))
             acc = product_mx("a_ps%d" % t, wo_code[:, cols], wo_scale[:, cols], 0)
-            for part in parts[t]:
+            for part in [first, second] if t == LANES - 1 else [whole]:
                 a_t = tile(label("a", t, part), [P, part.stop - part.start], F32)
                 nc.scalar.copy(a_t[:], acc[:, part])
-                a_sb[t, part.start] = a_t
+                for c in range(part.start, part.stop, half):
+                    a_sb[t, c, c + half] = a_t[:, c - part.start : c - part.start + half]
+                a_sb[t, part.start, part.stop] = a_t[:]
 
         u_code = tile("u_code", [P, LANES, P], I32)
         z_plane = [tile("z_plane%d" % c, [P, LANES, half], BF16) for c in range(2)]
         h_sq = {}
         total = {}
 
-        def gather_h(t, part, tag=None):
-            width = part.stop - part.start
-            h_t = tile(label("h", t, part), [P, width], F32, tag)
-            nc.vector.tensor_copy(h_t[:], listed(h_tab[t], part))
-            sq = tile(label("h_sq", t, part), [P, width], F32)
-            nc.scalar.activation(sq[:], h_t[:], ACT.Square)
+        def fresh(name, t, part, tag=None):
+            return tile(label(name, t, part), [P, part.stop - part.start], F32, tag)[:]
+
+        def gather_h(t, part, h_t):
+            nc.vector.tensor_copy(h_t, listed(h_tab[t], part))
+            sq = fresh("h_sq", t, part)
+            nc.scalar.activation(sq, h_t, ACT.Square)
             for c in range(part.start, part.stop, half):
                 h_sq[t, c] = sq[:, c - part.start : c - part.start + half]
 
-        def gather_dn(t, part, tag=None):
-            s = tile(label("total", t, part), [P, part.stop - part.start], F32, tag)
-            nc.vector.tensor_tensor(s[:], listed(dn_tab[t], part), a_sb[t, part.start][:], ALU.add)
+        def gather_dn(t, part, s):
+            nc.vector.tensor_tensor(s, listed(dn_tab[t], part), a_sb[t, part.start, part.stop], ALU.add)
             for c in range(part.start, part.stop, half):
                 total[t, c] = s[:, c - part.start : c - part.start + half]
 
@@ -142,24 +146,29 @@ def tile_attend_grnn_pl_kernel(tc, dy, wo, dn, hT, U_words, U_scales, offs, out_
             cols = slice(SLOTS + c, SLOTS + c + half)
             nc.vector.quantize_mx(grad_code[:, cols].bitcast(E5M2), grad_scale[:, cols], z_bf[:].rearrange("p i t -> p (i t)"))
 
-        gather_h(0, whole, "dy_bf")
         nc.vector.tensor_copy(u_code[:].rearrange("p t m -> p m t"), u_raw[:].rearrange("p (m t) -> p m t", t=LANES))
-        for t in range(2):
-            gather_dn(t, whole)
-            gather_h(t + 1, whole)
+        gather_h(0, whole, fresh("h", 0, whole, "dy_bf"))
+        gather_dn(0, whole, fresh("total", 0, whole))
+        gather_h(1, whole, fresh("h", 1, whole))
+        product(0, 0)
+        product(0, half)
+        for t in range(1, LANES):
+            gather_dn(t, first, fresh("total", t, first))
+            if t == 1:
+                gather_h(2, whole, fresh("h", 2, whole))
+            if t == 2:
+                gather_h(3, first, fresh("h", 3, first))
             product(t, 0)
-            product(t, half)
-        gather_dn(2, first)
-        gather_h(3, first)
-        product(2, 0)
-        gather_dn(3, first)
-        product(3, 0)
         z_first = weave_z(0)
-        gather_h(3, second, label("a", 3, first))
-        gather_dn(2, second, label("total", 3, first))
-        product(2, half)
+        before = tile("before", [P, 2, half], F32, label("a", 3, first))
+        gather_dn(1, second, before[:, 0, :])
+        gather_h(3, second, before[:, 1, :])
+        product(1, half)
         quantise_z(0, z_first)
-        gather_dn(3, second, "z_bf0")
+        after = tile("after", [P, 2, half], F32, "z_plane0")
+        gather_dn(2, second, after[:, 0, :])
+        gather_dn(3, second, after[:, 1, :])
+        product(2, half)
         product(3, half)
 
         def negated(t, part, acc, cols, tag=None):
@@ -204,11 +213,13 @@ def tile_attend_grnn_pl_kernel(tc, dy, wo, dn, hT, U_words, U_scales, offs, out_
                 nc.scalar.copy(y_bf[:, TAIL_VECTOR:, t], window[t][:, TAIL_VECTOR:])
 
         last = window[LANES - 1]
-        nc.vector.tensor_copy(y_pair[:, 1, :], last[:, :TAIL_VECTOR])
-        for c in range(TAIL_VECTOR, SESSIONS, CHUNK):
-            nc.scalar.copy(y_bf[:, c : c + CHUNK, LANES - 1], last[:, c : c + CHUNK])
-        for c in range(0, TAIL_VECTOR, CHUNK):
-            nc.vector.tensor_copy(y_bf[:, c : c + CHUNK, 2:4], y_pair[:, :, c : c + CHUNK].rearrange("p t c -> p c t"))
+        on_vector = (slice(0, CHUNK), slice(CHUNK, TAIL_VECTOR))
+        for cols in on_vector:
+            nc.vector.tensor_copy(y_pair[:, 1, cols], last[:, cols])
+        for cols in (slice(2 * CHUNK, 3 * CHUNK), slice(TAIL_VECTOR, 2 * CHUNK), slice(3 * CHUNK, SESSIONS)):
+            nc.scalar.copy(y_bf[:, cols, LANES - 1], last[:, cols])
+        for cols in on_vector:
+            nc.vector.tensor_copy(y_bf[:, cols, 2:4], y_pair[:, :, cols].rearrange("p t c -> p c t"))
 
         y_code = tile("y_code", [P, SESSIONS], I32)
         y_scale = tile("y_scale", [P, SESSIONS], U8)

@@ -19,10 +19,11 @@ SLOTS = 512
 SESSIONS = 1024
 FLOPS = 2 * 2 * D * D * SLOTS
 
-WO_VECTOR = 88
-DY_VECTOR = 352
+WO_VECTOR = 96
+DY_VECTOR = 416
 TAIL_VECTOR = 448
 CHUNK = 256
+PAIRED = 768
 
 
 def tile_attend_grnn_pl_kernel(tc, dy, wo, dn, hT, U_words, U_scales, offs, out_0, out_1, out_2):
@@ -79,9 +80,12 @@ def tile_attend_grnn_pl_kernel(tc, dy, wo, dn, hT, U_words, U_scales, offs, out_
         for u in range(2):
             dy_src = dy_raw[u][:].rearrange("p j i -> p i j")
             lanes = slice(2 * u, 2 * u + 2)
-            nc.scalar.copy(dy_bf[:, DY_VECTOR:, lanes], dy_src[:, DY_VECTOR:])
-            nc.vector.tensor_copy(dy_bf[:, :half, lanes], dy_src[:, :half])
-            nc.vector.tensor_copy(dy_bf[:, half:DY_VECTOR, lanes], dy_src[:, half:DY_VECTOR])
+            if u == 0:
+                nc.scalar.copy(dy_bf[:, :, lanes], dy_src)
+            else:
+                nc.scalar.copy(dy_bf[:, DY_VECTOR:, lanes], dy_src[:, DY_VECTOR:])
+                nc.vector.tensor_copy(dy_bf[:, :half, lanes], dy_src[:, :half])
+                nc.vector.tensor_copy(dy_bf[:, half:DY_VECTOR, lanes], dy_src[:, half:DY_VECTOR])
         grad_code = tile("grad_code", [P, 2 * SLOTS], I32)
         grad_scale = tile("grad_scale", [P, 2 * SLOTS], U8)
         for c in (0, half):
@@ -195,19 +199,16 @@ def tile_attend_grnn_pl_kernel(tc, dy, wo, dn, hT, U_words, U_scales, offs, out_
 
         out_rows = out_0.rearrange("(p t) c -> p t c", t=LANES)
         y_bf = tile("y_bf", [P, SESSIONS, LANES], BF16, "wo_bf")
-        y_low = tile("y_low", [P, 2, SESSIONS], BF16, "u_code")
+        y_low = tile("y_low", [P, 2, PAIRED], BF16, "u_code")
         y_pair = tile("y_pair", [P, 2, TAIL_VECTOR], BF16, "grad_scale")
         for t in range(LANES):
             scatter(t, rest[t], dh[t])
             nc.sync.dma_start(out_rows[:, t, :], window[t][:])
-            if t == 0:
-                nc.scalar.copy(y_low[:, t, :], window[t][:])
+            if t < 2:
+                nc.scalar.copy(y_low[:, t, :], window[t][:, :PAIRED])
+                nc.scalar.copy(y_bf[:, PAIRED:, t], window[t][:, PAIRED:])
             if t == 1:
-                sides = (slice(0, SESSIONS // 2), slice(SESSIONS // 2, SESSIONS))
-                for cols in sides:
-                    nc.scalar.copy(y_low[:, t, cols], window[t][:, cols])
-                for cols in sides:
-                    nc.scalar.copy(y_bf[:, cols, 0:2], y_low[:, :, cols].rearrange("p t c -> p c t"))
+                nc.scalar.copy(y_bf[:, :PAIRED, 0:2], y_low[:].rearrange("p t c -> p c t"))
             if t == 2:
                 nc.scalar.copy(y_pair[:, 0, :], window[t][:, :TAIL_VECTOR])
                 nc.scalar.copy(y_bf[:, TAIL_VECTOR:, t], window[t][:, TAIL_VECTOR:])

from contextlib import ExitStack

import concourse.mybir as mybir

F32 = mybir.dt.float32
BF16 = mybir.dt.bfloat16
I32 = mybir.dt.int32
U16 = mybir.dt.uint16
U8 = mybir.dt.uint8
E4M3 = mybir.dt.float8_e4m3fn_x4
E5M2 = mybir.dt.float8_e5m2_x4
ALU = mybir.AluOpType
ACT = mybir.ActivationFunctionType

P = 128
LANES = 4
D = 512
SLOTS = 512
SESSIONS = 1024
FLOPS = 2 * 2 * D * D * SLOTS

WO_VECTOR = 96
DY_VECTOR = 416
TAIL_VECTOR = 448
CHUNK = 256
PAIRED = 768


def tile_attend_grnn_pl_kernel(tc, dy, wo, dn, hT, U_words, U_scales, offs, out_0, out_1, out_2):
    nc = tc.nc
    with ExitStack() as ctx:
        sb = ctx.enter_context(tc.tile_pool(name="sb", bufs=1))
        ps = ctx.enter_context(tc.psum_pool(name="ps", bufs=1))

        def tile(name, shape, dtype, tag=None):
            return sb.tile(shape, dtype, name=name, tag=tag or name, align_bytes=64)

        offsets = sb.tile([P, SLOTS // 16], U16, name="offsets")
        nc.sync.dma_start(offsets[:], offs)

        wo_raw = tile("wo_raw", [P, LANES, D], F32)
        nc.sync.dma_start(wo_raw[:], wo.rearrange("(p j) h -> p j h", j=LANES))
        us_raw = tile("us_raw", [P, D], U8)
        nc.gpsimd.memset(us_raw[:].bitcast(I32), 0)
        for q in range(4):
            nc.scalar.dma_start(us_raw[32 * q : 32 * q + 4, :].bitcast(I32), U_scales[0, 4 * q : 4 * q + 4, :].bitcast(I32))
        dy_rows = dy.rearrange("(p j) i -> p j i", j=LANES)
        dy_raw = [tile("dy_raw%d" % u, [P, 2, SLOTS], F32) for u in range(2)]
        for u in range(2):
            nc.sync.dma_start(dy_raw[u][:], dy_rows[:, 2 * u : 2 * u + 2, :])

        h_rows = hT.rearrange("(p t) c -> p t c", t=LANES)
        dn_rows = dn.rearrange("(p t) c -> p t c", t=LANES)
        h_tab = [tile("h_tab%d" % t, [P, SESSIONS], F32) for t in range(LANES)]
        dn_tab = [tile("dn_tab%d" % t, [P, SESSIONS], F32) for t in range(LANES)]
        u_raw = tile("u_raw", [P, D], I32)
        nc.sync.dma_start(u_raw[:], U_words[0].rearrange("p k l -> p (k l)").bitcast(I32))
        for t in range(LANES):
            nc.sync.dma_start(h_tab[t][:], h_rows[:, t, :])
            nc.sync.dma_start(dn_tab[t][:], dn_rows[:, t, :])

        window = [tile("window%d" % t, [P, SESSIONS], F32) for t in range(LANES)]
        for t in range(LANES):
            nc.vector.memset(window[t][:], 0.0)

        wo_bf = tile("wo_bf", [P, LANES, P, LANES], BF16)
        wo_dst = wo_bf[:].rearrange("p t m j -> p m t j")
        wo_src = wo_raw[:].rearrange("p j (m t) -> p m t j", t=LANES)
        nc.vector.tensor_copy(wo_dst[:, :WO_VECTOR], wo_src[:, :WO_VECTOR])
        nc.scalar.copy(wo_dst[:, WO_VECTOR:], wo_src[:, WO_VECTOR:])
        wo_code = tile("wo_code", [P, D], I32)
        wo_scale = tile("wo_scale", [P, D], U8)
        nc.vector.quantize_mx(wo_code[:].bitcast(E4M3), wo_scale[:], wo_bf[:].rearrange("p t m j -> p (t m j)"))

        u_scale = tile("u_scale", [P, LANES, P], U8, "wo_bf")
        nc.vector.tensor_copy(u_scale[:].rearrange("p t m -> p m t"), us_raw[:].rearrange("p (m t) -> p m t", t=LANES))

        dy_bf = tile("dy_bf", [P, SLOTS, LANES], BF16)
        half = SLOTS // 2
        for u in range(2):
            dy_src = dy_raw[u][:].rearrange("p j i -> p i j")
            lanes = slice(2 * u, 2 * u + 2)
            if u == 0:
                nc.scalar.copy(dy_bf[:, :, lanes], dy_src)
            else:
                nc.scalar.copy(dy_bf[:, DY_VECTOR:, lanes], dy_src[:, DY_VECTOR:])
                nc.vector.tensor_copy(dy_bf[:, :half, lanes], dy_src[:, :half])
                nc.vector.tensor_copy(dy_bf[:, half:DY_VECTOR, lanes], dy_src[:, half:DY_VECTOR])
        grad_code = tile("grad_code", [P, 2 * SLOTS], I32)
        grad_scale = tile("grad_scale", [P, 2 * SLOTS], U8)
        for c in (0, half):
            cols = slice(c, c + half)
            nc.vector.quantize_mx(grad_code[:, cols].bitcast(E5M2), grad_scale[:, cols], dy_bf[:, cols, :].rearrange("p i j -> p (i j)"))

        first, second, whole = slice(0, half), slice(half, SLOTS), slice(0, SLOTS)

        def listed(table, part):
            return table[:].indirect(offsets[:, part.start // 16 : part.stop // 16])

        def label(name, t, part):
            return "%s%d_%d_%d" % (name, t, part.start, part.stop)

        def product_mx(name, code, scale, start):
            acc = ps.tile([P, SLOTS], F32, name=name, tag="bank", bufs=8)
            cols = slice(start, start + SLOTS)
            nc.tensor.matmul_mx(acc[:], lhsT=code.bitcast(E4M3), lhsT_scale=scale,
                                rhs=grad_code[:, cols].bitcast(E5M2), rhs_scale=grad_scale[:, cols], start=True, stop=True)
            return acc

        a_sb = {}
        for t in range(LANES):
            cols = slice(P * t, P * (t + 1))
            acc = product_mx("a_ps%d" % t, wo_code[:, cols], wo_scale[:, cols], 0)
            for part in [first, second] if t == LANES - 1 else [whole]:
                a_t = tile(label("a", t, part), [P, part.stop - part.start], F32)
                nc.scalar.copy(a_t[:], acc[:, part])
                for c in range(part.start, part.stop, half):
                    a_sb[t, c, c + half] = a_t[:, c - part.start : c - part.start + half]
                a_sb[t, part.start, part.stop] = a_t[:]

        u_code = tile("u_code", [P, LANES, P], I32)
        z_plane = [tile("z_plane%d" % c, [P, LANES, half], BF16) for c in range(2)]
        h_sq = {}
        total = {}

        def fresh(name, t, part, tag=None):
            return tile(label(name, t, part), [P, part.stop - part.start], F32, tag)[:]

        def gather_h(t, part, h_t):
            nc.vector.tensor_copy(h_t, listed(h_tab[t], part))
            sq = fresh("h_sq", t, part)
            nc.scalar.activation(sq, h_t, ACT.Square)
            for c in range(part.start, part.stop, half):
                h_sq[t, c] = sq[:, c - part.start : c - part.start + half]

        def gather_dn(t, part, s):
            nc.vector.tensor_tensor(s, listed(dn_tab[t], part), a_sb[t, part.start, part.stop], ALU.add)
            for c in range(part.start, part.stop, half):
                total[t, c] = s[:, c - part.start : c - part.start + half]

        def product(t, c):
            nc.vector.scalar_tensor_tensor(z_plane[c // half][:, t, :], h_sq[t, c], 1.0, total[t, c], ALU.subtract, ALU.mult)

        def weave_z(c):
            z_bf = tile("z_bf%d" % c, [P, half, LANES], BF16)
            nc.scalar.copy(z_bf[:], z_plane[c // half][:].rearrange("p t i -> p i t"))
            return z_bf

        def quantise_z(c, z_bf):
            cols = slice(SLOTS + c, SLOTS + c + half)
            nc.vector.quantize_mx(grad_code[:, cols].bitcast(E5M2), grad_scale[:, cols], z_bf[:].rearrange("p i t -> p (i t)"))

        nc.vector.tensor_copy(u_code[:].rearrange("p t m -> p m t"), u_raw[:].rearrange("p (m t) -> p m t", t=LANES))
        gather_h(0, whole, fresh("h", 0, whole, "dy_bf"))
        gather_dn(0, whole, fresh("total", 0, whole))
        gather_h(1, whole, fresh("h", 1, whole))
        product(0, 0)
        product(0, half)
        for t in range(1, LANES):
            gather_dn(t, first, fresh("total", t, first))
            if t == 1:
                gather_h(2, whole, fresh("h", 2, whole))
            if t == 2:
                gather_h(3, first, fresh("h", 3, first))
            product(t, 0)
        z_first = weave_z(0)
        before = tile("before", [P, 2, half], F32, label("a", 3, first))
        gather_dn(1, second, before[:, 0, :])
        gather_h(3, second, before[:, 1, :])
        product(1, half)
        quantise_z(0, z_first)
        after = tile("after", [P, 2, half], F32, "z_plane0")
        gather_dn(2, second, after[:, 0, :])
        gather_dn(3, second, after[:, 1, :])
        product(2, half)
        product(3, half)

        def negated(t, part, acc, cols, tag=None):
            dh_t = tile(label("dh", t, part), [P, part.stop - part.start], F32, tag)
            nc.scalar.activation(dh_t[:], acc[:, cols], ACT.Copy, scale=-1.0)
            return dh_t

        def scatter(t, part, dh_t):
            nc.vector.tensor_copy(listed(window[t], part), dh_t[:])

        early = [product_mx("early%d" % t, u_code[:, t, :], u_scale[:, t, :], half) for t in range(2)]
        dh_0 = negated(0, first, early[0], second)
        z_second = weave_z(half)
        dh_1 = negated(1, first, early[1], second, "z_plane1")
        scatter(0, first, dh_0)
        quantise_z(half, z_second)
        scatter(1, first, dh_1)

        rest = [second, second, whole, whole]
        dh = []
        for t in range(LANES):
            acc = product_mx("dh_ps%d" % t, u_code[:, t, :], u_scale[:, t, :], SLOTS)
            dh.append(negated(t, rest[t], acc, rest[t]))

        out_rows = out_0.rearrange("(p t) c -> p t c", t=LANES)
        y_bf = tile("y_bf", [P, SESSIONS, LANES], BF16, "wo_bf")
        y_low = tile("y_low", [P, 2, PAIRED], BF16, "u_code")
        y_pair = tile("y_pair", [P, 2, TAIL_VECTOR], BF16, "grad_scale")
        for t in range(LANES):
            scatter(t, rest[t], dh[t])
            nc.sync.dma_start(out_rows[:, t, :], window[t][:])
            if t < 2:
                nc.scalar.copy(y_low[:, t, :], window[t][:, :PAIRED])
                nc.scalar.copy(y_bf[:, PAIRED:, t], window[t][:, PAIRED:])
            if t == 1:
                nc.scalar.copy(y_bf[:, :PAIRED, 0:2], y_low[:].rearrange("p t c -> p c t"))
            if t == 2:
                nc.scalar.copy(y_pair[:, 0, :], window[t][:, :TAIL_VECTOR])
                nc.scalar.copy(y_bf[:, TAIL_VECTOR:, t], window[t][:, TAIL_VECTOR:])

        last = window[LANES - 1]
        on_vector = (slice(0, CHUNK), slice(CHUNK, TAIL_VECTOR))
        for cols in on_vector:
            nc.vector.tensor_copy(y_pair[:, 1, cols], last[:, cols])
        for cols in (slice(2 * CHUNK, 3 * CHUNK), slice(TAIL_VECTOR, 2 * CHUNK), slice(3 * CHUNK, SESSIONS)):
            nc.scalar.copy(y_bf[:, cols, LANES - 1], last[:, cols])
        for cols in on_vector:
            nc.vector.tensor_copy(y_bf[:, cols, 2:4], y_pair[:, :, cols].rearrange("p t c -> p c t"))

        y_code = tile("y_code", [P, SESSIONS], I32)
        y_scale = tile("y_scale", [P, SESSIONS], U8)
        word_rows = out_1[0].rearrange("p c l -> p (c l)").bitcast(I32)
        for c in (2 * CHUNK, 0, CHUNK, 3 * CHUNK):
            cols = slice(c, c + CHUNK)
            nc.vector.quantize_mx(y_code[:, cols].bitcast(E4M3), y_scale[:, cols], y_bf[:, cols, :].rearrange("p c t -> p (c t)"))
            nc.sync.dma_start(word_rows[:, cols], y_code[:, cols])
        for q in range(4):
            queue = nc.scalar if q % 2 else nc.sync
            queue.dma_start(out_2[0, 4 * q : 4 * q + 4, :].bitcast(I32), y_scale[32 * q : 32 * q + 4, :].bitcast(I32))
